import numpy as np
import ml_dtypes


def mxq(x, axis, fmt="e4m3"):
    dtype, down = {"e4m3": (ml_dtypes.float8_e4m3fn, 7), "e5m2": (ml_dtypes.float8_e5m2, 14)}[fmt]
    v = np.moveaxis(np.asarray(x, np.float32).astype(ml_dtypes.bfloat16).astype(np.float64), axis, -1)
    blocks = v.reshape(v.shape[:-1] + (-1, 32))
    amax = np.abs(blocks).max(-1, keepdims=True)
    byte = np.maximum(np.where(amax > 0, np.frexp(amax)[1] - 1 + 127, 0) - down, 1)
    scale = np.exp2(byte - 127.0)
    codes = (blocks / scale).astype(np.float32).astype(dtype).astype(np.float64)
    return np.moveaxis((codes * scale).reshape(v.shape), -1, axis)


WIDE = False


def mx_kscale(k):
    if not WIDE:
        return np.ones(k)
    levels = np.array([10, -10, 5, -5, 0])
    if k % 512:
        return np.exp2(np.random.permutation(np.resize(levels, k // 32))).repeat(32)
    a = np.empty((k // 512, 16))
    for p in range(k // 512):
        a[p, :8] = np.random.permutation(np.resize(levels, 8))
        for g in range(8):
            far = levels[np.abs(levels - a[p, g]) >= 10]
            a[p, g + 8] = far[np.random.randint(len(far))]
    return np.exp2(a.ravel()).repeat(32)


def f64(x):
    return np.asarray(x).astype(np.float64)


def striped(idx):
    return np.tile(idx.reshape(-1, 16).T, (8, 1)).astype(np.uint16)


def unstriped(offs):
    return offs[:16].T.reshape(-1).astype(np.int64)


E2M1 = np.array([0.0, 0.5, 1.0, 1.5, 2.0, 3.0, 4.0, 6.0, -0.0, -0.5, -1.0, -1.5, -2.0, -3.0, -4.0, -6.0])


def pack_weight(w, fmt):
    k, n = w.shape
    w = f64(np.asarray(w, np.float32).astype(ml_dtypes.bfloat16)).reshape(k // 32, 32, n)
    amax = np.abs(w).max(1)
    if fmt == "e4m3":
        byte = np.frexp(amax)[1] - 1 + 127 - 7
    else:
        mant, ex = np.frexp(amax / 6.0)
        byte = np.where(mant > 0.5, ex, ex - 1) + 127
    byte = np.clip(np.where(amax > 0, byte, 1), 1, 254)
    scaled = (w * np.exp2(127.0 - byte)[:, None, :]).reshape(k, n).astype(np.float32)
    by_word = np.ascontiguousarray(scaled.reshape(k // 512, 128, 4, n).transpose(0, 1, 3, 2))
    if fmt == "e4m3":
        words = by_word.astype(ml_dtypes.float8_e4m3fn).view(np.uint8)
    else:
        c = by_word.astype(ml_dtypes.float4_e2m1fn).view(np.uint8) & 0xF
        words = (c[..., 0::2] | (c[..., 1::2] << 4)).reshape(k // 512, 128, 2 * n)
    return np.ascontiguousarray(words), np.ascontiguousarray(byte.astype(np.uint8).reshape(k // 512, 16, n))


def unpack_weight(words, scales, fmt):
    g, _, n = scales.shape
    words = np.ascontiguousarray(words).reshape(g, 128, n, -1)
    if fmt == "e4m3":
        vals = words.view(ml_dtypes.float8_e4m3fn).astype(np.float64)
    else:
        nib = np.empty((g, 128, n, 4), np.uint8)
        nib[..., 0::2] = words & 0xF
        nib[..., 1::2] = words >> 4
        vals = E2M1[nib]
    vals = vals * np.repeat(np.exp2(scales.astype(np.float64) - 127.0), 8, axis=1)[..., None]
    return vals.transpose(0, 1, 3, 2).reshape(g * 512, n)


def gelu(v):
    return 0.5 * v * (1.0 + np.tanh(np.sqrt(2.0 / np.pi) * (v + 0.044715 * v**3)))


def bf(x):
    return np.asarray(x, np.float32).astype(ml_dtypes.bfloat16)


def planes(Y):
    n, m = Y.shape
    b = f64(bf(Y)).reshape(n // 32, 32, m)
    amax = np.abs(b).max(1)
    byte = np.clip(np.where(amax > 0, np.frexp(amax)[1] - 1 + 127 - 7, 1), 1, 254)
    codes = (b * np.exp2(127.0 - byte)[:, None, :]).reshape(n, m).astype(np.float32).astype(ml_dtypes.float8_e4m3fn).view(np.uint8)
    words = codes.reshape(n // 512, 128, 4, m).transpose(0, 1, 3, 2)
    return np.ascontiguousarray(words), np.ascontiguousarray(byte.astype(np.uint8).reshape(n // 512, 16, m))


K, H, N, T, S, T2, P = 512, 1024, 768, 4096, 1024, 2048, 1024

def setup_inputs():
    n = np.random.standard_normal
    s = mx_kscale(K)[:, None]
    u = mx_kscale(H)[:, None]
    d = {}
    d["tab_words"], d["tab_scales"] = pack_weight(n((K, T)) * s, "e4m3")
    d["offs"] = striped(np.random.permutation(T)[:S])
    d["offs2"] = striped(np.random.permutation(T2)[:S])
    d["offs3"] = striped(np.random.permutation(T2)[:P])
    d["w1"] = (n((K, H)) / K ** 0.5 / s * u.T).astype(np.float32)
    d["w2_words"], d["w2_scales"] = pack_weight(1.4 * n((K, H)) / K ** 0.5 / s * u.T, "e2m1")
    d["wgs"] = np.exp(0.3 * n((128, S))).astype(np.float32)
    d["page0"] = (n((H, T2)) * u).astype(np.float32)
    d["gain"] = np.random.uniform(0.4, 1.6, H).astype(np.float32)
    d["bz"] = (0.6 * n(H) * u[:, 0]).astype(np.float32)
    d["w3"] = (n((H, N)) / H ** 0.5 / u).astype(np.float32)
    d["bather"] = np.random.uniform(0.4, 1.6, (N, P)).astype(np.float32)
    d["base"] = (0.7 * n((N, P))).astype(np.float32)
    return d

def reference(tab_words, tab_scales, offs, offs2, offs3, w1, w2_words, w2_scales, wgs, page0, gain, bz, w3, bather, base):
    v = unpack_weight(tab_words, tab_scales, "e4m3")[:, unstriped(offs)]
    w2 = unpack_weight(w2_words, w2_scales, "e2m1")
    a = mxq(f64(w1), 0, "e4m3").T @ v
    b = w2.T @ v
    h = np.maximum(np.abs(a), b)
    page = f64(page0).copy()
    page[:, unstriped(offs2)] = np.tile(f64(wgs), (H // 128, 1)) * h
    x = page[:, unstriped(offs3)]
    z = x * f64(gain)[:, None] + f64(bz)[:, None]
    e = mxq(f64(w3), 0, "e4m3").T @ mxq(z, 0, "e4m3")
    y = e * f64(bather) + f64(base)
    words, scales = planes(page)
    return y, page, words, scales

@@ -1,0 +1,334 @@
+from contextlib import ExitStack
+from functools import partial
+
+import concourse.mybir as mybir
+from concourse.masks import make_identity
+
+K, H, N, T, S, T2, J = 512, 1024, 768, 4096, 1024, 2048, 1024
+FLOPS = 2 * (2 * K * H * S + H * N * J)
+
+F32 = mybir.dt.float32
+BF16 = mybir.dt.bfloat16
+I32 = mybir.dt.int32
+U32 = mybir.dt.uint32
+U16 = mybir.dt.uint16
+U8 = mybir.dt.uint8
+FP8X4 = mybir.dt.float8_e4m3fn_x4
+FP4X4 = mybir.dt.float4_e2m1fn_x4
+ACT = mybir.ActivationFunctionType
+ALU = mybir.AluOpType
+
+P = 128
+BANK = 512
+ROW_BLOCKS = H // P
+GROUPS = H // 512
+N_BLOCKS = N // P
+W1_PIECES = ((0, 256), (256, 256), (512, 512))
+
+
+def tile_list_pool_test_page_kernel(
+    tc, tab_words, tab_scales, offs, offs2, offs3, w1, w2_words, w2_scales, wgs, page0, gain, bz, w3, bather, base,
+    out_0, out_1, out_2, out_3,
+):
+    nc = tc.nc
+    with ExitStack() as ctx:
+        keep = ctx.enter_context(tc.tile_pool(name="keep", bufs=1))
+        work = ctx.enter_context(tc.tile_pool(name="work", bufs=2))
+        psum = ctx.enter_context(tc.psum_pool(name="psum", bufs=2))
+
+        idx1 = keep.tile([P, S // 16], U16, name="idx1")
+        idx2 = keep.tile([P, S // 16], U16, name="idx2")
+        idx3 = keep.tile([P, J // 16], U16, name="idx3")
+        v_codes = keep.tile([P, S], U32, name="v_codes", align_bytes=64)
+        v_scales = keep.tile([P, S], U8, name="v_scales", align_bytes=64)
+        w1_codes = keep.tile([P, H], U32, name="w1_codes", align_bytes=64)
+        w1_scales = keep.tile([P, H], U8, name="w1_scales", align_bytes=64)
+        w2_codes = keep.tile([P, 2 * H], U8, name="w2_codes", align_bytes=64)
+        w2_sc = keep.tile([P, H], U8, name="w2_sc", align_bytes=64)
+        wgs_sb = keep.tile([P, S], F32, name="wgs_sb")
+        ident_f = keep.tile([P, P], F32, name="ident_f")
+        ident_b = keep.tile([P, P], BF16, name="ident_b")
+        vec_rows = keep.tile([P, P], F32, name="vec_rows")
+        vec_cols = keep.tile([P, 2 * ROW_BLOCKS], F32, name="vec_cols")
+        w3_codes = [keep.tile([P, N], U32, name="w3_codes%d" % g, align_bytes=64) for g in range(GROUPS)]
+        w3_scales = [keep.tile([P, N], U8, name="w3_scales%d" % g, align_bytes=64) for g in range(GROUPS)]
+        z_codes = [[keep.tile([P, BANK], U32, name="z_codes%d%d" % (g, h), align_bytes=64) for h in range(2)] for g in range(GROUPS)]
+        z_scales = [[keep.tile([P, BANK], U8, name="z_scales%d%d" % (g, h), align_bytes=64) for h in range(2)] for g in range(GROUPS)]
+
+        tab_w = work.tile([P, T], I32, name="tab_w", tag="big", align_bytes=64)
+        w1_raw = work.tile([P, 4 * H], F32, name="w1_raw", tag="big", align_bytes=64)
+        tab_s = work.tile([P, T], U8, name="tab_s", tag="x", align_bytes=64)
+
+        def load_scale_rows(tile, rows):
+            for q in range(4):
+                nc.sync.dma_start(out=tile[32 * q : 32 * q + 4, :].bitcast(I32), in_=rows[4 * q : 4 * q + 4, :].bitcast(I32))
+
+        def round_and_group(raw, width):
+            grouped = work.tile([P, width, 4], BF16, name="grouped", tag="grouped", align_bytes=64)
+            nc.scalar.copy(
+                out=grouped[:].rearrange("p (c i) t -> p c t i", i=4), in_=raw.rearrange("p t (c i) -> p c t i", i=4)
+            )
+            return grouped[:].rearrange("p c t -> p (c t)")
+
+        def quantize(codes, scales, grouped):
+            nc.vector.quantize_mx(out=codes.bitcast(FP8X4), scales=scales, in_=grouped)
+
+        def w1_view(c0, width):
+            return w1_raw[:, 4 * c0 : 4 * (c0 + width)].rearrange("p (t c) -> p t c", t=4)
+
+        def load_w1(c0, width):
+            nc.sync.dma_start(out=w1_view(c0, width), in_=w1[:, c0 : c0 + width].rearrange("(p t) c -> p t c", t=4))
+
+        def quantize_w1(c0, width):
+            grouped = round_and_group(w1_view(c0, width), width)
+            quantize(w1_codes[:, c0 : c0 + width], w1_scales[:, c0 : c0 + width], grouped)
+
+        pages = {}
+
+        def load_page(c):
+            pages[c] = work.tile([P, T2], F32, name="page", tag="page", bufs=7)
+            nc.sync.dma_start(out=pages[c][:], in_=page0[P * c : P * (c + 1), :])
+
+        w3_raw = {}
+
+        def load_w3(g):
+            w3_raw[g] = work.tile([P, 4, N], F32, name="w3_raw", tag="wide")
+            nc.sync.dma_start(out=w3_raw[g][:], in_=w3[512 * g : 512 * (g + 1), :].rearrange("(p t) n -> p t n", t=4))
+
+        nc.vector.memset(tab_s[:].bitcast(I32), 0)
+        nc.vector.memset(w2_sc[:].bitcast(I32), 0)
+        nc.sync.dma_start(out=idx1[:], in_=offs)
+        load_w1(*W1_PIECES[0])
+        load_scale_rows(tab_s, tab_scales[0])
+        nc.sync.dma_start(out=w2_codes[:].bitcast(I32), in_=w2_words[0].bitcast(I32))
+        nc.sync.dma_start(out=tab_w[:], in_=tab_words[0].rearrange("p t i -> p (t i)").bitcast(I32))
+        load_scale_rows(w2_sc, w2_scales[0])
+        nc.sync.dma_start(out=idx2[:], in_=offs2)
+        nc.sync.dma_start(out=wgs_sb[:], in_=wgs)
+        load_page(0)
+        nc.sync.dma_start(out=idx3[:], in_=offs3)
+        load_w1(*W1_PIECES[1])
+        load_page(1)
+        load_w1(*W1_PIECES[2])
+        load_page(2)
+        load_w3(0)
+        load_page(3)
+        load_w3(1)
+        for c in range(4, 7):
+            load_page(c)
+
+        make_identity(nc, ident_f[:])
+        make_identity(nc, ident_b[:])
+        nc.gpsimd.memset(vec_rows[:], 0.0)
+        nc.gpsimd.dma_start(out=vec_rows[0:ROW_BLOCKS, :], in_=gain.rearrange("(c q) -> c q", q=P))
+        nc.gpsimd.dma_start(out=vec_rows[ROW_BLOCKS : 2 * ROW_BLOCKS, :], in_=bz.rearrange("(c q) -> c q", q=P))
+
+        quantize_w1(*W1_PIECES[0])
+        nc.vector.tensor_copy(out=v_scales[:], in_=tab_s[:].indirect(idx1[:]))
+        for h in range(2):
+            nc.vector.tensor_copy(
+                out=v_codes[:, BANK * h : BANK * (h + 1)], in_=tab_w[:].bitcast(U32).indirect(idx1[:, 32 * h : 32 * (h + 1)])
+            )
+
+        hs = {}
+        b_banks = {}
+
+        def products(c):
+            hs[c] = work.tile([P, S], F32, name="h", tag="h", bufs=3)
+            for h in range(2):
+                cols = slice(BANK * h, BANK * (h + 1))
+                a_bank = psum.tile([P, BANK], F32, name="a_bank", tag="a")
+                b_banks[c, h] = psum.tile([P, BANK], F32, name="b_bank", tag="b")
+                nc.tensor.matmul_mx(
+                    out=a_bank[:], lhsT=w1_codes[:, P * c : P * (c + 1)].bitcast(FP8X4), lhsT_scale=w1_scales[:, P * c : P * (c + 1)],
+                    rhs=v_codes[:, cols].bitcast(FP8X4), rhs_scale=v_scales[:, cols], start=True, stop=True,
+                )
+                nc.tensor.matmul_mx(
+                    out=b_banks[c, h][:], lhsT=w2_codes[:, 2 * P * c : 2 * P * (c + 1)].bitcast(FP4X4), lhsT_scale=w2_sc[:, P * c : P * (c + 1)],
+                    rhs=v_codes[:, cols].bitcast(FP8X4), rhs_scale=v_scales[:, cols], start=True, stop=True,
+                )
+                nc.scalar.activation(out=hs[c][:, cols], in_=a_bank[:], func=ACT.Abs)
+
+        def maximum(c, h):
+            cols = slice(BANK * h, BANK * (h + 1))
+            nc.vector.tensor_tensor(out=hs[c][:, cols], in0=b_banks[c, h][:], in1=hs[c][:, cols], op=ALU.max)
+
+        def scatter(c, j0, j1):
+            nc.vector.tensor_tensor(
+                out=pages[c][:].indirect(idx2[:, j0 // 16 : j1 // 16]), in0=hs[c][:, j0:j1], in1=wgs_sb[:, j0:j1], op=ALU.mult
+            )
+
+        xs = {}
+
+        def gather(c, j0, j1):
+            if j0 == 0:
+                xs[c] = work.tile([P, J], F32, name="x", tag="x", align_bytes=64)
+            nc.vector.tensor_copy(out=xs[c][:, j0:j1], in_=pages[c][:].indirect(idx3[:, j0 // 16 : j1 // 16]))
+
+        page_t = {}
+
+        def turn_page(c):
+            g, cc = divmod(c, 4)
+            if cc == 0:
+                page_t[g] = work.tile([P, T2 // P, 2, P, 2], BF16, name="page_t", tag="big", align_bytes=64)
+            for m4 in range(T2 // BANK):
+                bank = psum.tile([P, 4, P], F32, name="f_bank", tag="f")
+                for b in range(4):
+                    m0 = BANK * m4 + P * b
+                    nc.tensor.transpose(bank[:, b, :], pages[c][:, m0 : m0 + P], ident_f[:])
+                nc.scalar.copy(
+                    out=page_t[g][:, 4 * m4 : 4 * m4 + 4, :, 32 * cc : 32 * cc + 32, :],
+                    in_=bank[:].rearrange("m b (p u e) -> m b u p e", u=2, e=2),
+                )
+
+        def turn_back(words, blocks, tag):
+            grouped = work.tile([P, P * len(blocks), 2], F32, name="back", tag=tag, align_bytes=64)
+            for i in range(0, len(blocks), 2):
+                bank = psum.tile([P, 2, 2 * P], F32, name="r_bank", tag="r")
+                for b in range(2):
+                    for u in range(2):
+                        nc.tensor.transpose(bank[:, u, P * b : P * (b + 1)], words[:, blocks[i + b], u, :], ident_f[:])
+                nc.scalar.copy(out=grouped[:, P * i : P * (i + 2), :], in_=bank[:].rearrange("p u m -> p m u"))
+            return grouped[:].rearrange("p m u -> p (m u)").bitcast(BF16)
+
+        z_t = {}
+
+        def turn_z(c, h):
+            g, cc = divmod(c, 4)
+            if cc == 0:
+                z_t[g, h] = work.tile([P, 4, 2, P], F32, name="z_t", tag="z_t")
+            cols = slice(BANK * h, BANK * (h + 1))
+            z_rows = work.tile([P, BANK], BF16, name="z_rows", tag="z_rows", bufs=3)
+            nc.scalar.activation(
+                out=z_rows[:], in_=xs[c][:, cols], func=ACT.Identity,
+                scale=vec_cols[:, c : c + 1], bias=vec_cols[:, ROW_BLOCKS + c : ROW_BLOCKS + c + 1],
+            )
+            bank = psum.tile([P, 4, P], BF16, name="z_bank", tag="f")
+            for b in range(4):
+                nc.tensor.transpose(bank[:, b, :], z_rows[:, P * b : P * (b + 1)], ident_b[:])
+            nc.scalar.copy(
+                out=z_t[g, h][:, :, :, 32 * cc : 32 * cc + 32],
+                in_=bank[:].bitcast(F32).rearrange("j b (p u) -> j b u p", u=2),
+            )
+
+        plane_codes = {}
+        plane_scales = {}
+
+        def planes_back(g, m4):
+            words = page_t[g][:].rearrange("m b u p e -> m b u (p e)").bitcast(F32)
+            return turn_back(words, list(range(4 * m4, 4 * m4 + 4)), "plane_in")
+
+        def planes_quantize(g, m4, grouped, queue):
+            if m4 == 0:
+                plane_codes[g] = work.tile([P, T2], U32, name="plane_codes", tag="plane_codes", align_bytes=64)
+                plane_scales[g] = work.tile([P, T2], U8, name="plane_scales", tag="plane_scales", align_bytes=64)
+            cols = slice(BANK * m4, BANK * (m4 + 1))
+            quantize(plane_codes[g][:, cols], plane_scales[g][:, cols], grouped)
+            if m4 % 2 == 1:
+                cols = slice(BANK * (m4 - 1), BANK * (m4 + 1))
+                queue.dma_start(
+                    out=out_2[g].rearrange("p m t -> p (m t)").bitcast(I32)[:, cols], in_=plane_codes[g][:, cols].bitcast(I32)
+                )
+            if m4 == T2 // BANK - 1:
+                for q in range(4):
+                    queue.dma_start(
+                        out=out_3[g, 4 * q : 4 * q + 4, :].bitcast(I32), in_=plane_scales[g][32 * q : 32 * q + 4, :].bitcast(I32)
+                    )
+
+        def quantize_w3(g):
+            grouped = round_and_group(w3_raw[g][:], N)
+            quantize(w3_codes[g][:, 0:512], w3_scales[g][:, 0:512], grouped[:, 0:2048])
+            quantize(w3_codes[g][:, 512:N], w3_scales[g][:, 512:N], grouped[:, 2048 : 4 * N])
+
+        bathers = {}
+        bases = {}
+
+        def load_bather(i):
+            bathers[i] = work.tile([P, 3, J], F32, name="bather_sb", tag="wide")
+            nc.sync.dma_start(out=bathers[i][:], in_=bather[3 * P * i : 3 * P * (i + 1), :].rearrange("(b p) j -> p b j", p=P))
+
+        def load_base(i):
+            bases[i] = work.tile([P, 2, J], F32, name="base_sb", tag="page", bufs=7)
+            nc.sync.dma_start(out=bases[i][:], in_=base[2 * P * i : 2 * P * (i + 1), :].rearrange("(b p) j -> p b j", p=P))
+
+        products(0)
+        vec_bank = psum.tile([P, P], F32, name="vec_bank", tag="r")
+        nc.tensor.transpose(vec_bank[:], vec_rows[:], ident_f[:])
+        nc.scalar.copy(out=vec_cols[:], in_=vec_bank[:, 0 : 2 * ROW_BLOCKS])
+        maximum(0, 0)
+        maximum(0, 1)
+        products(1)
+
+        last = ROW_BLOCKS - 1
+        waiting = []
+        for c in range(ROW_BLOCKS):
+            if c == 0:
+                scatter(c, 0, BANK)
+                scatter(c, BANK, S)
+            else:
+                scatter(c, 0, S)
+            (nc.sync if c == last else nc.gpsimd).dma_start(out=out_1[P * c : P * (c + 1), :], in_=pages[c][:])
+            if c == 0:
+                quantize_w1(*W1_PIECES[1])
+            if c == 1:
+                quantize_w1(*W1_PIECES[2])
+            if c < last:
+                maximum(c + 1, 0)
+                maximum(c + 1, 1)
+                for job in waiting:
+                    job()
+                waiting.clear()
+                gather(c, 0, J)
+                if c + 2 < ROW_BLOCKS:
+                    products(c + 2)
+                turn_page(c)
+                turn_z(c, 0)
+                turn_z(c, 1)
+            if c == 0:
+                load_page(7)
+            if c in (1, 2):
+                quantize_w3(c - 1)
+                load_bather(c - 1)
+            if c in (1, 2, 3):
+                load_base(c - 1)
+            if c == 3:
+                for h in range(2):
+                    grouped = turn_back(z_t[0, h][:], list(range(4)), "grouped")
+                    waiting.append(partial(quantize, z_codes[0][h][:], z_scales[0][h][:], grouped))
+            if c in (4, 5):
+                for m4 in range(2 * (c - 4), 2 * (c - 4) + 2):
+                    waiting.append(partial(planes_quantize, 0, m4, planes_back(0, m4), nc.gpsimd))
+
+        for h in range(2):
+            gather(last, BANK * h, BANK * (h + 1))
+        for h in range(2):
+            turn_z(last, h)
+            quantize(z_codes[1][h][:], z_scales[1][h][:], turn_back(z_t[1, h][:], list(range(4)), "grouped"))
+        turn_page(last)
+
+        def score(h, nb):
+            cols = slice(BANK * h, BANK * (h + 1))
+            bank = psum.tile([P, BANK], F32, name="e_bank", tag="ab"[nb % 2])
+            for g in range(GROUPS):
+                nc.tensor.matmul_mx(
+                    out=bank[:], lhsT=w3_codes[g][:, P * nb : P * (nb + 1)].bitcast(FP8X4), lhsT_scale=w3_scales[g][:, P * nb : P * (nb + 1)],
+                    rhs=z_codes[g][h][:].bitcast(FP8X4), rhs_scale=z_scales[g][h][:], start=(g == 0), stop=(g == GROUPS - 1),
+                )
+            scaled = bathers[nb // 3][:, nb % 3, cols]
+            nc.vector.tensor_tensor(out=scaled, in0=bank[:], in1=scaled, op=ALU.mult)
+
+        def finish(h, nb):
+            cols = slice(BANK * h, BANK * (h + 1))
+            y = bases[nb // 2][:, nb % 2, cols]
+            nc.vector.tensor_tensor(out=y, in0=bathers[nb // 3][:, nb % 3, cols], in1=y, op=ALU.add)
+            nc.sync.dma_start(out=out_0[P * nb : P * (nb + 1), cols], in_=y)
+
+        units = [(h, nb) for h in range(2) for nb in range(N_BLOCKS)]
+        for i, unit in enumerate(units):
+            score(*unit)
+            if i > 0:
+                finish(*units[i - 1])
+            if i in (3, 5, 7, 9):
+                m4 = (i - 3) // 2
+                planes_quantize(1, m4, planes_back(1, m4), nc.sync)
+        finish(*units[-1])

@@ -46,6 +46,7 @@ def tile_list_pool_test_page_kernel(
         w2_codes = keep.tile([P, 2 * H], U8, name="w2_codes", align_bytes=64)
         w2_sc = keep.tile([P, H], U8, name="w2_sc", align_bytes=64)
         wgs_sb = keep.tile([P, S], F32, name="wgs_sb")
+        h_sb = keep.tile([P, S], F32, name="h_sb")
         ident_f = keep.tile([P, P], F32, name="ident_f")
         ident_b = keep.tile([P, P], BF16, name="ident_b")
         vec_rows = keep.tile([P, P], F32, name="vec_rows")
@@ -63,12 +64,10 @@ def tile_list_pool_test_page_kernel(
             for q in range(4):
                 nc.sync.dma_start(out=tile[32 * q : 32 * q + 4, :].bitcast(I32), in_=rows[4 * q : 4 * q + 4, :].bitcast(I32))
 
-        def round_and_group(raw, width):
-            grouped = work.tile([P, width, 4], BF16, name="grouped", tag="grouped", align_bytes=64)
+        def round_and_group(raw, grouped):
             nc.scalar.copy(
-                out=grouped[:].rearrange("p (c i) t -> p c t i", i=4), in_=raw.rearrange("p t (c i) -> p c t i", i=4)
+                out=grouped.rearrange("p (c i t) -> p c t i", i=4, t=4), in_=raw.rearrange("p t (c i) -> p c t i", i=4)
             )
-            return grouped[:].rearrange("p c t -> p (c t)")
 
         def quantize(codes, scales, grouped):
             nc.vector.quantize_mx(out=codes.bitcast(FP8X4), scales=scales, in_=grouped)
@@ -79,9 +78,10 @@ def tile_list_pool_test_page_kernel(
         def load_w1(c0, width):
             nc.sync.dma_start(out=w1_view(c0, width), in_=w1[:, c0 : c0 + width].rearrange("(p t) c -> p t c", t=4))
 
-        def quantize_w1(c0, width):
-            grouped = round_and_group(w1_view(c0, width), width)
-            quantize(w1_codes[:, c0 : c0 + width], w1_scales[:, c0 : c0 + width], grouped)
+        def quantize_w1(piece, grouped):
+            c0, width = W1_PIECES[piece]
+            round_and_group(w1_view(c0, width), grouped)
+            return partial(quantize, w1_codes[:, c0 : c0 + width], w1_scales[:, c0 : c0 + width], grouped)
 
         pages = {}
 
@@ -97,19 +97,23 @@ def tile_list_pool_test_page_kernel(
 
         nc.vector.memset(tab_s[:].bitcast(I32), 0)
         nc.vector.memset(w2_sc[:].bitcast(I32), 0)
+        w2_in = w2_words[0].bitcast(I32)
+        first = 4 * P // 4
         nc.sync.dma_start(out=idx1[:], in_=offs)
         load_w1(*W1_PIECES[0])
+        nc.sync.dma_start(out=w2_codes[:].bitcast(I32)[:, :first], in_=w2_in[:, :first])
         load_scale_rows(tab_s, tab_scales[0])
-        nc.sync.dma_start(out=w2_codes[:].bitcast(I32), in_=w2_words[0].bitcast(I32))
         nc.sync.dma_start(out=tab_w[:], in_=tab_words[0].rearrange("p t i -> p (t i)").bitcast(I32))
         load_scale_rows(w2_sc, w2_scales[0])
         nc.sync.dma_start(out=idx2[:], in_=offs2)
-        nc.sync.dma_start(out=wgs_sb[:], in_=wgs)
+        nc.sync.dma_start(out=wgs_sb[:, :BANK], in_=wgs[:, :BANK])
         load_page(0)
+        nc.sync.dma_start(out=wgs_sb[:, BANK:], in_=wgs[:, BANK:])
         nc.sync.dma_start(out=idx3[:], in_=offs3)
         load_w1(*W1_PIECES[1])
-        load_page(1)
+        nc.sync.dma_start(out=w2_codes[:].bitcast(I32)[:, first:], in_=w2_in[:, first:])
         load_w1(*W1_PIECES[2])
+        load_page(1)
         load_page(2)
         load_w3(0)
         load_page(3)
@@ -118,23 +122,24 @@ def tile_list_pool_test_page_kernel(
             load_page(c)
 
         make_identity(nc, ident_f[:])
-        make_identity(nc, ident_b[:])
+        nc.scalar.copy(out=ident_b[:], in_=ident_f[:])
         nc.gpsimd.memset(vec_rows[:], 0.0)
         nc.gpsimd.dma_start(out=vec_rows[0:ROW_BLOCKS, :], in_=gain.rearrange("(c q) -> c q", q=P))
         nc.gpsimd.dma_start(out=vec_rows[ROW_BLOCKS : 2 * ROW_BLOCKS, :], in_=bz.rearrange("(c q) -> c q", q=P))
 
-        quantize_w1(*W1_PIECES[0])
-        nc.vector.tensor_copy(out=v_scales[:], in_=tab_s[:].indirect(idx1[:]))
+        first_grouped = work.tile([P, 4 * W1_PIECES[0][1]], BF16, name="first_grouped", tag="grouped", align_bytes=64)
+        quantize_w1(0, first_grouped[:])()
         for h in range(2):
+            nc.vector.tensor_copy(out=v_scales[:, BANK * h : BANK * (h + 1)], in_=tab_s[:].indirect(idx1[:, 32 * h : 32 * (h + 1)]))
             nc.vector.tensor_copy(
                 out=v_codes[:, BANK * h : BANK * (h + 1)], in_=tab_w[:].bitcast(U32).indirect(idx1[:, 32 * h : 32 * (h + 1)])
             )
 
-        hs = {}
+        mags = {}
         b_banks = {}
 
         def products(c):
-            hs[c] = work.tile([P, S], F32, name="h", tag="h", bufs=3)
+            mags[c] = work.tile([P, S], F32, name="mag", tag="mag", bufs=3, align_bytes=64)
             for h in range(2):
                 cols = slice(BANK * h, BANK * (h + 1))
                 a_bank = psum.tile([P, BANK], F32, name="a_bank", tag="a")
@@ -147,23 +152,27 @@ def tile_list_pool_test_page_kernel(
                     out=b_banks[c, h][:], lhsT=w2_codes[:, 2 * P * c : 2 * P * (c + 1)].bitcast(FP4X4), lhsT_scale=w2_sc[:, P * c : P * (c + 1)],
                     rhs=v_codes[:, cols].bitcast(FP8X4), rhs_scale=v_scales[:, cols], start=True, stop=True,
                 )
-                nc.scalar.activation(out=hs[c][:, cols], in_=a_bank[:], func=ACT.Abs)
+                nc.scalar.activation(out=mags[c][:, cols], in_=a_bank[:], func=ACT.Abs)
 
         def maximum(c, h):
             cols = slice(BANK * h, BANK * (h + 1))
-            nc.vector.tensor_tensor(out=hs[c][:, cols], in0=b_banks[c, h][:], in1=hs[c][:, cols], op=ALU.max)
+            nc.vector.tensor_tensor(out=h_sb[:, cols], in0=b_banks[c, h][:], in1=mags[c][:, cols], op=ALU.max)
 
         def scatter(c, j0, j1):
             nc.vector.tensor_tensor(
-                out=pages[c][:].indirect(idx2[:, j0 // 16 : j1 // 16]), in0=hs[c][:, j0:j1], in1=wgs_sb[:, j0:j1], op=ALU.mult
+                out=pages[c][:].indirect(idx2[:, j0 // 16 : j1 // 16]), in0=h_sb[:, j0:j1], in1=wgs_sb[:, j0:j1], op=ALU.mult
             )
 
         xs = {}
 
-        def gather(c, j0, j1):
-            if j0 == 0:
-                xs[c] = work.tile([P, J], F32, name="x", tag="x", align_bytes=64)
-            nc.vector.tensor_copy(out=xs[c][:, j0:j1], in_=pages[c][:].indirect(idx3[:, j0 // 16 : j1 // 16]))
+        def gather(c, j0, j1, into):
+            for h in range(j0 // BANK, j1 // BANK):
+                xs[c, h] = into[:, BANK * h - j0 : BANK * (h + 1) - j0]
+            nc.vector.tensor_copy(out=into, in_=pages[c][:].indirect(idx3[:, j0 // 16 : j1 // 16]))
+
+        def fresh_x(width):
+            x = work.tile([P, width], F32, name="x", tag="x", align_bytes=64)
+            return x[:]
 
         page_t = {}
 
@@ -197,10 +206,9 @@ def tile_list_pool_test_page_kernel(
             g, cc = divmod(c, 4)
             if cc == 0:
                 z_t[g, h] = work.tile([P, 4, 2, P], F32, name="z_t", tag="z_t")
-            cols = slice(BANK * h, BANK * (h + 1))
             z_rows = work.tile([P, BANK], BF16, name="z_rows", tag="z_rows", bufs=3)
             nc.scalar.activation(
-                out=z_rows[:], in_=xs[c][:, cols], func=ACT.Identity,
+                out=z_rows[:], in_=xs[c, h], func=ACT.Identity,
                 scale=vec_cols[:, c : c + 1], bias=vec_cols[:, ROW_BLOCKS + c : ROW_BLOCKS + c + 1],
             )
             bank = psum.tile([P, 4, P], BF16, name="z_bank", tag="f")
@@ -218,7 +226,7 @@ def tile_list_pool_test_page_kernel(
             words = page_t[g][:].rearrange("m b u p e -> m b u (p e)").bitcast(F32)
             return turn_back(words, list(range(4 * m4, 4 * m4 + 4)), "plane_in")
 
-        def planes_quantize(g, m4, grouped, queue):
+        def planes_quantize(g, m4, grouped):
             if m4 == 0:
                 plane_codes[g] = work.tile([P, T2], U32, name="plane_codes", tag="plane_codes", align_bytes=64)
                 plane_scales[g] = work.tile([P, T2], U8, name="plane_scales", tag="plane_scales", align_bytes=64)
@@ -226,19 +234,18 @@ def tile_list_pool_test_page_kernel(
             quantize(plane_codes[g][:, cols], plane_scales[g][:, cols], grouped)
             if m4 % 2 == 1:
                 cols = slice(BANK * (m4 - 1), BANK * (m4 + 1))
-                queue.dma_start(
+                nc.sync.dma_start(
                     out=out_2[g].rearrange("p m t -> p (m t)").bitcast(I32)[:, cols], in_=plane_codes[g][:, cols].bitcast(I32)
                 )
             if m4 == T2 // BANK - 1:
                 for q in range(4):
-                    queue.dma_start(
+                    nc.sync.dma_start(
                         out=out_3[g, 4 * q : 4 * q + 4, :].bitcast(I32), in_=plane_scales[g][32 * q : 32 * q + 4, :].bitcast(I32)
                     )
 
-        def quantize_w3(g):
-            grouped = round_and_group(w3_raw[g][:], N)
-            quantize(w3_codes[g][:, 0:512], w3_scales[g][:, 0:512], grouped[:, 0:2048])
-            quantize(w3_codes[g][:, 512:N], w3_scales[g][:, 512:N], grouped[:, 2048 : 4 * N])
+        def quantize_w3(g, n0, n1, grouped):
+            round_and_group(w3_raw[g][:, :, n0:n1], grouped)
+            return partial(quantize, w3_codes[g][:, n0:n1], w3_scales[g][:, n0:n1], grouped)
 
         bathers = {}
         bases = {}
@@ -251,71 +258,19 @@ def tile_list_pool_test_page_kernel(
             bases[i] = work.tile([P, 2, J], F32, name="base_sb", tag="page", bufs=7)
             nc.sync.dma_start(out=bases[i][:], in_=base[2 * P * i : 2 * P * (i + 1), :].rearrange("(b p) j -> p b j", p=P))
 
-        products(0)
-        vec_bank = psum.tile([P, P], F32, name="vec_bank", tag="r")
-        nc.tensor.transpose(vec_bank[:], vec_rows[:], ident_f[:])
-        nc.scalar.copy(out=vec_cols[:], in_=vec_bank[:, 0 : 2 * ROW_BLOCKS])
-        maximum(0, 0)
-        maximum(0, 1)
-        products(1)
+        e_banks = {}
 
-        last = ROW_BLOCKS - 1
-        waiting = []
-        for c in range(ROW_BLOCKS):
-            if c == 0:
-                scatter(c, 0, BANK)
-                scatter(c, BANK, S)
-            else:
-                scatter(c, 0, S)
-            (nc.sync if c == last else nc.gpsimd).dma_start(out=out_1[P * c : P * (c + 1), :], in_=pages[c][:])
-            if c == 0:
-                quantize_w1(*W1_PIECES[1])
-            if c == 1:
-                quantize_w1(*W1_PIECES[2])
-            if c < last:
-                maximum(c + 1, 0)
-                maximum(c + 1, 1)
-                for job in waiting:
-                    job()
-                waiting.clear()
-                gather(c, 0, J)
-                if c + 2 < ROW_BLOCKS:
-                    products(c + 2)
-                turn_page(c)
-                turn_z(c, 0)
-                turn_z(c, 1)
-            if c == 0:
-                load_page(7)
-            if c in (1, 2):
-                quantize_w3(c - 1)
-                load_bather(c - 1)
-            if c in (1, 2, 3):
-                load_base(c - 1)
-            if c == 3:
-                for h in range(2):
-                    grouped = turn_back(z_t[0, h][:], list(range(4)), "grouped")
-                    waiting.append(partial(quantize, z_codes[0][h][:], z_scales[0][h][:], grouped))
-            if c in (4, 5):
-                for m4 in range(2 * (c - 4), 2 * (c - 4) + 2):
-                    waiting.append(partial(planes_quantize, 0, m4, planes_back(0, m4), nc.gpsimd))
+        def score_pass(h, nb, g):
+            if g == 0:
+                e_banks[h, nb] = psum.tile([P, BANK], F32, name="e_bank", tag="ab"[nb % 2])
+            nc.tensor.matmul_mx(
+                out=e_banks[h, nb][:], lhsT=w3_codes[g][:, P * nb : P * (nb + 1)].bitcast(FP8X4), lhsT_scale=w3_scales[g][:, P * nb : P * (nb + 1)],
+                rhs=z_codes[g][h][:].bitcast(FP8X4), rhs_scale=z_scales[g][h][:], start=(g == 0), stop=(g == GROUPS - 1),
+            )
 
-        for h in range(2):
-            gather(last, BANK * h, BANK * (h + 1))
-        for h in range(2):
-            turn_z(last, h)
-            quantize(z_codes[1][h][:], z_scales[1][h][:], turn_back(z_t[1, h][:], list(range(4)), "grouped"))
-        turn_page(last)
-
-        def score(h, nb):
-            cols = slice(BANK * h, BANK * (h + 1))
-            bank = psum.tile([P, BANK], F32, name="e_bank", tag="ab"[nb % 2])
-            for g in range(GROUPS):
-                nc.tensor.matmul_mx(
-                    out=bank[:], lhsT=w3_codes[g][:, P * nb : P * (nb + 1)].bitcast(FP8X4), lhsT_scale=w3_scales[g][:, P * nb : P * (nb + 1)],
-                    rhs=z_codes[g][h][:].bitcast(FP8X4), rhs_scale=z_scales[g][h][:], start=(g == 0), stop=(g == GROUPS - 1),
-                )
-            scaled = bathers[nb // 3][:, nb % 3, cols]
-            nc.vector.tensor_tensor(out=scaled, in0=bank[:], in1=scaled, op=ALU.mult)
+        def weigh(h, nb):
+            scaled = bathers[nb // 3][:, nb % 3, BANK * h : BANK * (h + 1)]
+            nc.vector.tensor_tensor(out=scaled, in0=e_banks[h, nb][:], in1=scaled, op=ALU.mult)
 
         def finish(h, nb):
             cols = slice(BANK * h, BANK * (h + 1))
@@ -323,12 +278,88 @@ def tile_list_pool_test_page_kernel(
             nc.vector.tensor_tensor(out=y, in0=bathers[nb // 3][:, nb % 3, cols], in1=y, op=ALU.add)
             nc.sync.dma_start(out=out_0[P * nb : P * (nb + 1), cols], in_=y)
 
+        def quantize_z(g, h):
+            grouped = turn_back(z_t[g, h][:], list(range(4)), "grouped")
+            return partial(quantize, z_codes[g][h][:], z_scales[g][h][:], grouped)
+
+        products(0)
+        maximum(0, 0)
+        maximum(0, 1)
+        products(1)
+        vec_bank = psum.tile([P, P], F32, name="vec_bank", tag="r")
+        nc.tensor.transpose(vec_bank[:], vec_rows[:], ident_f[:])
+        nc.scalar.copy(out=vec_cols[:], in_=vec_bank[:, 0 : 2 * ROW_BLOCKS])
+
+        last = ROW_BLOCKS - 1
         units = [(h, nb) for h in range(2) for nb in range(N_BLOCKS)]
-        for i, unit in enumerate(units):
-            score(*unit)
+        opened = units[:4]
+        waiting = []
+        for c in range(ROW_BLOCKS):
+            if c == 0:
+                scatter(c, 0, BANK)
+                scatter(c, BANK, S)
+            else:
+                scatter(c, 0, S)
+            nc.sync.dma_start(out=out_1[P * c : P * (c + 1), :], in_=pages[c][:])
+            if c == last:
+                break
+            maximum(c + 1, 0)
+            maximum(c + 1, 1)
+            spent = mags[c + 1][:].bitcast(BF16)
+            weights = []
+            if c < 2:
+                weights.append(quantize_w1(c + 1, spent[:, : 4 * W1_PIECES[c + 1][1]]))
+            if c in (2, 4):
+                weights.append(quantize_w3(c // 2 - 1, 0, BANK, spent))
+            if c == 3:
+                weights.extend(quantize_w3(g, BANK, N, spent[:, 1024 * g : 1024 * (g + 1)]) for g in range(GROUPS))
+            for job in waiting:
+                job()
+            waiting.clear()
+            width = J if c < 4 else BANK
+            gather(c, 0, width, fresh_x(width))
+            for job in weights:
+                job()
+            if c + 2 < ROW_BLOCKS:
+                products(c + 2)
+            else:
+                for h, nb in opened:
+                    score_pass(h, nb, 0)
+            turn_page(c)
+            for h in range(width // BANK):
+                turn_z(c, h)
+            if c == 0:
+                load_page(last)
+            if c in (3, 4):
+                load_bather(c - 3)
+            if c in (1, 2, 3):
+                load_base(c - 1)
+            if c == 3:
+                waiting.extend(quantize_z(0, h) for h in range(2))
+            if c in (4, 5):
+                for m4 in range(2 * (c - 4), 2 * (c - 4) + 2):
+                    waiting.append(partial(planes_quantize, 0, m4, planes_back(0, m4)))
+
+        gather(last, 0, BANK, fresh_x(BANK))
+        turn_z(last, 0)
+        first_half = quantize_z(1, 0)
+        spare = [h_sb[:, :BANK], h_sb[:, BANK:], wgs_sb[:, :BANK], wgs_sb[:, BANK:]]
+        for c in range(4, ROW_BLOCKS):
+            gather(c, BANK, J, spare[c - 4])
+            turn_z(c, 1)
+        first_half()
+        second_half = quantize_z(1, 1)
+        turn_page(last)
+
+        for i, (h, nb) in enumerate(units):
+            if (h, nb) not in opened:
+                score_pass(h, nb, 0)
+            score_pass(h, nb, 1)
+            weigh(h, nb)
             if i > 0:
                 finish(*units[i - 1])
-            if i in (3, 5, 7, 9):
-                m4 = (i - 3) // 2
-                planes_quantize(1, m4, planes_back(1, m4), nc.sync)
+            if i == 2:
+                second_half()
+            if i in (4, 5, 6, 7):
+                planes_quantize(1, i - 4, planes_back(1, i - 4))
         finish(*units[-1])

from contextlib import ExitStack
from functools import partial

import concourse.mybir as mybir
from concourse.masks import make_identity

K, H, N, T, S, T2, J = 512, 1024, 768, 4096, 1024, 2048, 1024
FLOPS = 2 * (2 * K * H * S + H * N * J)

F32 = mybir.dt.float32
BF16 = mybir.dt.bfloat16
I32 = mybir.dt.int32
U32 = mybir.dt.uint32
U16 = mybir.dt.uint16
U8 = mybir.dt.uint8
FP8X4 = mybir.dt.float8_e4m3fn_x4
FP4X4 = mybir.dt.float4_e2m1fn_x4
ACT = mybir.ActivationFunctionType
ALU = mybir.AluOpType

P = 128
BANK = 512
ROW_BLOCKS = H // P
GROUPS = H // 512
N_BLOCKS = N // P
W1_PIECES = ((0, 256), (256, 256), (512, 512))


def tile_list_pool_test_page_kernel(
    tc, tab_words, tab_scales, offs, offs2, offs3, w1, w2_words, w2_scales, wgs, page0, gain, bz, w3, bather, base,
    out_0, out_1, out_2, out_3,
):
    nc = tc.nc
    with ExitStack() as ctx:
        keep = ctx.enter_context(tc.tile_pool(name="keep", bufs=1))
        work = ctx.enter_context(tc.tile_pool(name="work", bufs=2))
        psum = ctx.enter_context(tc.psum_pool(name="psum", bufs=2))

        idx1 = keep.tile([P, S // 16], U16, name="idx1")
        idx2 = keep.tile([P, S // 16], U16, name="idx2")
        idx3 = keep.tile([P, J // 16], U16, name="idx3")
        v_codes = keep.tile([P, S], U32, name="v_codes", align_bytes=64)
        v_scales = keep.tile([P, S], U8, name="v_scales", align_bytes=64)
        w1_codes = keep.tile([P, H], U32, name="w1_codes", align_bytes=64)
        w1_scales = keep.tile([P, H], U8, name="w1_scales", align_bytes=64)
        w2_codes = keep.tile([P, 2 * H], U8, name="w2_codes", align_bytes=64)
        w2_sc = keep.tile([P, H], U8, name="w2_sc", align_bytes=64)
        wgs_sb = keep.tile([P, S], F32, name="wgs_sb")
        h_sb = keep.tile([P, S], F32, name="h_sb")
        ident_f = keep.tile([P, P], F32, name="ident_f")
        ident_b = keep.tile([P, P], BF16, name="ident_b")
        vec_rows = keep.tile([P, P], F32, name="vec_rows")
        vec_cols = keep.tile([P, 2 * ROW_BLOCKS], F32, name="vec_cols")
        w3_codes = [keep.tile([P, N], U32, name="w3_codes%d" % g, align_bytes=64) for g in range(GROUPS)]
        w3_scales = [keep.tile([P, N], U8, name="w3_scales%d" % g, align_bytes=64) for g in range(GROUPS)]
        z_codes = [[keep.tile([P, BANK], U32, name="z_codes%d%d" % (g, h), align_bytes=64) for h in range(2)] for g in range(GROUPS)]
        z_scales = [[keep.tile([P, BANK], U8, name="z_scales%d%d" % (g, h), align_bytes=64) for h in range(2)] for g in range(GROUPS)]

        tab_w = work.tile([P, T], I32, name="tab_w", tag="big", align_bytes=64)
        w1_raw = work.tile([P, 4 * H], F32, name="w1_raw", tag="big", align_bytes=64)
        tab_s = work.tile([P, T], U8, name="tab_s", tag="x", align_bytes=64)

        def load_scale_rows(tile, rows):
            for q in range(4):
                nc.sync.dma_start(out=tile[32 * q : 32 * q + 4, :].bitcast(I32), in_=rows[4 * q : 4 * q + 4, :].bitcast(I32))

        def round_and_group(raw, grouped):
            nc.scalar.copy(
                out=grouped.rearrange("p (c i t) -> p c t i", i=4, t=4), in_=raw.rearrange("p t (c i) -> p c t i", i=4)
            )

        def quantize(codes, scales, grouped):
            nc.vector.quantize_mx(out=codes.bitcast(FP8X4), scales=scales, in_=grouped)

        def w1_view(c0, width):
            return w1_raw[:, 4 * c0 : 4 * (c0 + width)].rearrange("p (t c) -> p t c", t=4)

        def load_w1(c0, width):
            nc.sync.dma_start(out=w1_view(c0, width), in_=w1[:, c0 : c0 + width].rearrange("(p t) c -> p t c", t=4))

        def quantize_w1(piece, grouped):
            c0, width = W1_PIECES[piece]
            round_and_group(w1_view(c0, width), grouped)
            return partial(quantize, w1_codes[:, c0 : c0 + width], w1_scales[:, c0 : c0 + width], grouped)

        pages = {}

        def load_page(c):
            pages[c] = work.tile([P, T2], F32, name="page", tag="page", bufs=7)
            nc.sync.dma_start(out=pages[c][:], in_=page0[P * c : P * (c + 1), :])

        w3_raw = {}

        def load_w3(g):
            w3_raw[g] = work.tile([P, 4, N], F32, name="w3_raw", tag="wide")
            nc.sync.dma_start(out=w3_raw[g][:], in_=w3[512 * g : 512 * (g + 1), :].rearrange("(p t) n -> p t n", t=4))

        nc.vector.memset(tab_s[:].bitcast(I32), 0)
        nc.vector.memset(w2_sc[:].bitcast(I32), 0)
        w2_in = w2_words[0].bitcast(I32)
        first = 4 * P // 4
        nc.sync.dma_start(out=idx1[:], in_=offs)
        load_w1(*W1_PIECES[0])
        nc.sync.dma_start(out=w2_codes[:].bitcast(I32)[:, :first], in_=w2_in[:, :first])
        load_scale_rows(tab_s, tab_scales[0])
        nc.sync.dma_start(out=tab_w[:], in_=tab_words[0].rearrange("p t i -> p (t i)").bitcast(I32))
        load_scale_rows(w2_sc, w2_scales[0])
        nc.sync.dma_start(out=idx2[:], in_=offs2)
        nc.sync.dma_start(out=wgs_sb[:, :BANK], in_=wgs[:, :BANK])
        load_page(0)
        nc.sync.dma_start(out=wgs_sb[:, BANK:], in_=wgs[:, BANK:])
        nc.sync.dma_start(out=idx3[:], in_=offs3)
        load_w1(*W1_PIECES[1])
        nc.sync.dma_start(out=w2_codes[:].bitcast(I32)[:, first:], in_=w2_in[:, first:])
        load_w1(*W1_PIECES[2])
        load_page(1)
        load_page(2)
        load_w3(0)
        load_page(3)
        load_w3(1)
        for c in range(4, 7):
            load_page(c)

        make_identity(nc, ident_f[:])
        nc.scalar.copy(out=ident_b[:], in_=ident_f[:])
        nc.gpsimd.memset(vec_rows[:], 0.0)
        nc.gpsimd.dma_start(out=vec_rows[0:ROW_BLOCKS, :], in_=gain.rearrange("(c q) -> c q", q=P))
        nc.gpsimd.dma_start(out=vec_rows[ROW_BLOCKS : 2 * ROW_BLOCKS, :], in_=bz.rearrange("(c q) -> c q", q=P))

        first_grouped = work.tile([P, 4 * W1_PIECES[0][1]], BF16, name="first_grouped", tag="grouped", align_bytes=64)
        quantize_w1(0, first_grouped[:])()
        for h in range(2):
            nc.vector.tensor_copy(out=v_scales[:, BANK * h : BANK * (h + 1)], in_=tab_s[:].indirect(idx1[:, 32 * h : 32 * (h + 1)]))
            nc.vector.tensor_copy(
                out=v_codes[:, BANK * h : BANK * (h + 1)], in_=tab_w[:].bitcast(U32).indirect(idx1[:, 32 * h : 32 * (h + 1)])
            )

        mags = {}
        b_banks = {}

        def products(c):
            mags[c] = work.tile([P, S], F32, name="mag", tag="mag", bufs=3, align_bytes=64)
            for h in range(2):
                cols = slice(BANK * h, BANK * (h + 1))
                a_bank = psum.tile([P, BANK], F32, name="a_bank", tag="a")
                b_banks[c, h] = psum.tile([P, BANK], F32, name="b_bank", tag="b")
                nc.tensor.matmul_mx(
                    out=a_bank[:], lhsT=w1_codes[:, P * c : P * (c + 1)].bitcast(FP8X4), lhsT_scale=w1_scales[:, P * c : P * (c + 1)],
                    rhs=v_codes[:, cols].bitcast(FP8X4), rhs_scale=v_scales[:, cols], start=True, stop=True,
                )
                nc.tensor.matmul_mx(
                    out=b_banks[c, h][:], lhsT=w2_codes[:, 2 * P * c : 2 * P * (c + 1)].bitcast(FP4X4), lhsT_scale=w2_sc[:, P * c : P * (c + 1)],
                    rhs=v_codes[:, cols].bitcast(FP8X4), rhs_scale=v_scales[:, cols], start=True, stop=True,
                )
                nc.scalar.activation(out=mags[c][:, cols], in_=a_bank[:], func=ACT.Abs)

        def maximum(c, h):
            cols = slice(BANK * h, BANK * (h + 1))
            nc.vector.tensor_tensor(out=h_sb[:, cols], in0=b_banks[c, h][:], in1=mags[c][:, cols], op=ALU.max)

        def scatter(c, j0, j1):
            nc.vector.tensor_tensor(
                out=pages[c][:].indirect(idx2[:, j0 // 16 : j1 // 16]), in0=h_sb[:, j0:j1], in1=wgs_sb[:, j0:j1], op=ALU.mult
            )

        xs = {}

        def gather(c, j0, j1, into):
            for h in range(j0 // BANK, j1 // BANK):
                xs[c, h] = into[:, BANK * h - j0 : BANK * (h + 1) - j0]
            nc.vector.tensor_copy(out=into, in_=pages[c][:].indirect(idx3[:, j0 // 16 : j1 // 16]))

        def fresh_x(width):
            x = work.tile([P, width], F32, name="x", tag="x", align_bytes=64)
            return x[:]

        page_t = {}

        def turn_page(c):
            g, cc = divmod(c, 4)
            if cc == 0:
                page_t[g] = work.tile([P, T2 // P, 2, P, 2], BF16, name="page_t", tag="big", align_bytes=64)
            for m4 in range(T2 // BANK):
                bank = psum.tile([P, 4, P], F32, name="f_bank", tag="f")
                for b in range(4):
                    m0 = BANK * m4 + P * b
                    nc.tensor.transpose(bank[:, b, :], pages[c][:, m0 : m0 + P], ident_f[:])
                nc.scalar.copy(
                    out=page_t[g][:, 4 * m4 : 4 * m4 + 4, :, 32 * cc : 32 * cc + 32, :],
                    in_=bank[:].rearrange("m b (p u e) -> m b u p e", u=2, e=2),
                )

        def turn_back(words, blocks, tag):
            grouped = work.tile([P, P * len(blocks), 2], F32, name="back", tag=tag, align_bytes=64)
            for i in range(0, len(blocks), 2):
                bank = psum.tile([P, 2, 2 * P], F32, name="r_bank", tag="r")
                for b in range(2):
                    for u in range(2):
                        nc.tensor.transpose(bank[:, u, P * b : P * (b + 1)], words[:, blocks[i + b], u, :], ident_f[:])
                nc.scalar.copy(out=grouped[:, P * i : P * (i + 2), :], in_=bank[:].rearrange("p u m -> p m u"))
            return grouped[:].rearrange("p m u -> p (m u)").bitcast(BF16)

        z_t = {}

        def turn_z(c, h):
            g, cc = divmod(c, 4)
            if cc == 0:
                z_t[g, h] = work.tile([P, 4, 2, P], F32, name="z_t", tag="z_t")
            z_rows = work.tile([P, BANK], BF16, name="z_rows", tag="z_rows", bufs=3)
            nc.scalar.activation(
                out=z_rows[:], in_=xs[c, h], func=ACT.Identity,
                scale=vec_cols[:, c : c + 1], bias=vec_cols[:, ROW_BLOCKS + c : ROW_BLOCKS + c + 1],
            )
            bank = psum.tile([P, 4, P], BF16, name="z_bank", tag="f")
            for b in range(4):
                nc.tensor.transpose(bank[:, b, :], z_rows[:, P * b : P * (b + 1)], ident_b[:])
            nc.scalar.copy(
                out=z_t[g, h][:, :, :, 32 * cc : 32 * cc + 32],
                in_=bank[:].bitcast(F32).rearrange("j b (p u) -> j b u p", u=2),
            )

        plane_codes = {}
        plane_scales = {}

        def planes_back(g, m4):
            words = page_t[g][:].rearrange("m b u p e -> m b u (p e)").bitcast(F32)
            return turn_back(words, list(range(4 * m4, 4 * m4 + 4)), "plane_in")

        def planes_quantize(g, m4, grouped):
            if m4 == 0:
                plane_codes[g] = work.tile([P, T2], U32, name="plane_codes", tag="plane_codes", align_bytes=64)
                plane_scales[g] = work.tile([P, T2], U8, name="plane_scales", tag="plane_scales", align_bytes=64)
            cols = slice(BANK * m4, BANK * (m4 + 1))
            quantize(plane_codes[g][:, cols], plane_scales[g][:, cols], grouped)
            if m4 % 2 == 1:
                cols = slice(BANK * (m4 - 1), BANK * (m4 + 1))
                nc.sync.dma_start(
                    out=out_2[g].rearrange("p m t -> p (m t)").bitcast(I32)[:, cols], in_=plane_codes[g][:, cols].bitcast(I32)
                )
            if m4 == T2 // BANK - 1:
                for q in range(4):
                    nc.sync.dma_start(
                        out=out_3[g, 4 * q : 4 * q + 4, :].bitcast(I32), in_=plane_scales[g][32 * q : 32 * q + 4, :].bitcast(I32)
                    )

        def quantize_w3(g, n0, n1, grouped):
            round_and_group(w3_raw[g][:, :, n0:n1], grouped)
            return partial(quantize, w3_codes[g][:, n0:n1], w3_scales[g][:, n0:n1], grouped)

        bathers = {}
        bases = {}

        def load_bather(i):
            bathers[i] = work.tile([P, 3, J], F32, name="bather_sb", tag="wide")
            nc.sync.dma_start(out=bathers[i][:], in_=bather[3 * P * i : 3 * P * (i + 1), :].rearrange("(b p) j -> p b j", p=P))

        def load_base(i):
            bases[i] = work.tile([P, 2, J], F32, name="base_sb", tag="page", bufs=7)
            nc.sync.dma_start(out=bases[i][:], in_=base[2 * P * i : 2 * P * (i + 1), :].rearrange("(b p) j -> p b j", p=P))

        e_banks = {}

        def score_pass(h, nb, g):
            if g == 0:
                e_banks[h, nb] = psum.tile([P, BANK], F32, name="e_bank", tag="ab"[nb % 2])
            nc.tensor.matmul_mx(
                out=e_banks[h, nb][:], lhsT=w3_codes[g][:, P * nb : P * (nb + 1)].bitcast(FP8X4), lhsT_scale=w3_scales[g][:, P * nb : P * (nb + 1)],
                rhs=z_codes[g][h][:].bitcast(FP8X4), rhs_scale=z_scales[g][h][:], start=(g == 0), stop=(g == GROUPS - 1),
            )

        def weigh(h, nb):
            scaled = bathers[nb // 3][:, nb % 3, BANK * h : BANK * (h + 1)]
            nc.vector.tensor_tensor(out=scaled, in0=e_banks[h, nb][:], in1=scaled, op=ALU.mult)

        def finish(h, nb):
            cols = slice(BANK * h, BANK * (h + 1))
            y = bases[nb // 2][:, nb % 2, cols]
            nc.vector.tensor_tensor(out=y, in0=bathers[nb // 3][:, nb % 3, cols], in1=y, op=ALU.add)
            nc.sync.dma_start(out=out_0[P * nb : P * (nb + 1), cols], in_=y)

        def quantize_z(g, h):
            grouped = turn_back(z_t[g, h][:], list(range(4)), "grouped")
            return partial(quantize, z_codes[g][h][:], z_scales[g][h][:], grouped)

        products(0)
        maximum(0, 0)
        maximum(0, 1)
        products(1)
        vec_bank = psum.tile([P, P], F32, name="vec_bank", tag="r")
        nc.tensor.transpose(vec_bank[:], vec_rows[:], ident_f[:])
        nc.scalar.copy(out=vec_cols[:], in_=vec_bank[:, 0 : 2 * ROW_BLOCKS])

        last = ROW_BLOCKS - 1
        units = [(h, nb) for h in range(2) for nb in range(N_BLOCKS)]
        opened = units[:4]
        waiting = []
        for c in range(ROW_BLOCKS):
            if c == 0:
                scatter(c, 0, BANK)
                scatter(c, BANK, S)
            else:
                scatter(c, 0, S)
            nc.sync.dma_start(out=out_1[P * c : P * (c + 1), :], in_=pages[c][:])
            if c == last:
                break
            maximum(c + 1, 0)
            maximum(c + 1, 1)
            spent = mags[c + 1][:].bitcast(BF16)
            weights = []
            if c < 2:
                weights.append(quantize_w1(c + 1, spent[:, : 4 * W1_PIECES[c + 1][1]]))
            if c in (2, 4):
                weights.append(quantize_w3(c // 2 - 1, 0, BANK, spent))
            if c == 3:
                weights.extend(quantize_w3(g, BANK, N, spent[:, 1024 * g : 1024 * (g + 1)]) for g in range(GROUPS))
            for job in waiting:
                job()
            waiting.clear()
            width = J if c < 4 else BANK
            gather(c, 0, width, fresh_x(width))
            for job in weights:
                job()
            if c + 2 < ROW_BLOCKS:
                products(c + 2)
            else:
                for h, nb in opened:
                    score_pass(h, nb, 0)
            turn_page(c)
            for h in range(width // BANK):
                turn_z(c, h)
            if c == 0:
                load_page(last)
            if c in (3, 4):
                load_bather(c - 3)
            if c in (1, 2, 3):
                load_base(c - 1)
            if c == 3:
                waiting.extend(quantize_z(0, h) for h in range(2))
            if c in (4, 5):
                for m4 in range(2 * (c - 4), 2 * (c - 4) + 2):
                    waiting.append(partial(planes_quantize, 0, m4, planes_back(0, m4)))

        gather(last, 0, BANK, fresh_x(BANK))
        turn_z(last, 0)
        first_half = quantize_z(1, 0)
        spare = [h_sb[:, :BANK], h_sb[:, BANK:], wgs_sb[:, :BANK], wgs_sb[:, BANK:]]
        for c in range(4, ROW_BLOCKS):
            gather(c, BANK, J, spare[c - 4])
            turn_z(c, 1)
        first_half()
        second_half = quantize_z(1, 1)
        turn_page(last)

        for i, (h, nb) in enumerate(units):
            if (h, nb) not in opened:
                score_pass(h, nb, 0)
            score_pass(h, nb, 1)
            weigh(h, nb)
            if i > 0:
                finish(*units[i - 1])
            if i == 2:
                second_half()
            if i in (4, 5, 6, 7):
                planes_quantize(1, i - 4, planes_back(1, i - 4))
        finish(*units[-1])
